import numpy as np
import ml_dtypes


def mxq(x, axis, fmt="e4m3"):
    dtype, down = {"e4m3": (ml_dtypes.float8_e4m3fn, 7), "e5m2": (ml_dtypes.float8_e5m2, 14)}[fmt]
    v = np.moveaxis(np.asarray(x, np.float32).astype(ml_dtypes.bfloat16).astype(np.float64), axis, -1)
    blocks = v.reshape(v.shape[:-1] + (-1, 32))
    amax = np.abs(blocks).max(-1, keepdims=True)
    byte = np.maximum(np.where(amax > 0, np.frexp(amax)[1] - 1 + 127, 0) - down, 1)
    scale = np.exp2(byte - 127.0)
    codes = (blocks / scale).astype(np.float32).astype(dtype).astype(np.float64)
    return np.moveaxis((codes * scale).reshape(v.shape), -1, axis)


WIDE = False


def mx_kscale(k):
    if not WIDE:
        return np.ones(k)
    levels = np.array([10, -10, 5, -5, 0])
    if k % 512:
        return np.exp2(np.random.permutation(np.resize(levels, k // 32))).repeat(32)
    a = np.empty((k // 512, 16))
    for p in range(k // 512):
        a[p, :8] = np.random.permutation(np.resize(levels, 8))
        for g in range(8):
            far = levels[np.abs(levels - a[p, g]) >= 10]
            a[p, g + 8] = far[np.random.randint(len(far))]
    return np.exp2(a.ravel()).repeat(32)


def f64(x):
    return np.asarray(x).astype(np.float64)


def striped(idx):
    return np.tile(idx.reshape(-1, 16).T, (8, 1)).astype(np.uint16)


def unstriped(offs):
    return offs[:16].T.reshape(-1).astype(np.int64)


def striped8(idx):
    return np.concatenate([x.reshape(-1, 16).T for x in idx]).astype(np.uint16)


def runs(offs, k):
    lists = np.stack([offs[16 * r : 16 * r + 16].T.reshape(-1) for r in range(8)]).astype(np.int64)
    return lists[np.arange(k) % 512 // 64]


def pack_weight(w):
    k, n = w.shape
    w = f64(np.asarray(w, np.float32).astype(ml_dtypes.bfloat16)).reshape(k // 32, 32, n)
    amax = np.abs(w).max(1)
    byte = np.clip(np.where(amax > 0, np.frexp(amax)[1] - 1 + 127 - 7, 1), 1, 254)
    scaled = (w * np.exp2(127.0 - byte)[:, None, :]).reshape(k, n).astype(np.float32)
    words = np.ascontiguousarray(scaled.reshape(k // 512, 128, 4, n).transpose(0, 1, 3, 2)).astype(ml_dtypes.float8_e4m3fn).view(np.uint8)
    return words, np.ascontiguousarray(byte.astype(np.uint8).reshape(k // 512, 16, n))


def unpack_weight(words, scales):
    g, p, n, _ = words.shape
    vals = np.ascontiguousarray(words).view(ml_dtypes.float8_e4m3fn).astype(np.float64) * np.repeat(np.exp2(scales.astype(np.float64) - 127.0), 8, axis=1)[..., None]
    return vals.transpose(0, 1, 3, 2).reshape(g * 512, n)

def planes(y):
    n, m = y.shape
    v = y.astype(np.float32).astype(ml_dtypes.bfloat16).astype(np.float64).reshape(n // 32, 32, m)
    top = np.abs(v).max(1)
    byte = np.clip(np.where(top > 0, np.frexp(top)[1] - 1 + 127 - 7, 1), 1, 254)
    codes = (v * np.exp2(127.0 - byte)[:, None, :]).reshape(n, m).astype(np.float32).astype(ml_dtypes.float8_e4m3fn).view(np.uint8)
    words = codes.reshape(n // 512, 128, 4, m).transpose(0, 1, 3, 2)
    return np.ascontiguousarray(words), np.ascontiguousarray(byte.astype(np.uint8).reshape(n // 512, 16, m))


K, T, S, G, H, W, C = 512, 1024, 512, 2048, 512, 384, 512


def setup_inputs():
    n = np.random.standard_normal
    s = mx_kscale(K)[:, None]
    packed_xT = pack_weight(n((K, T)) * s)
    packed_dT = pack_weight(n((K, G)) / s)
    return {
        "x_words": packed_xT[0],
        "x_scales": packed_xT[1],
        "d_words": packed_dT[0],
        "d_scales": packed_dT[1],
        "gs": (np.random.uniform(0.5, 1.5, (K, 1)) / s).astype(np.float32),
        "tau": np.random.uniform(0.3, 0.9, (H, 1)).astype(np.float32),
        "offs": striped(np.random.permutation(T)[:S]),
        "k1": striped8(np.random.randint(0, G, (8, H))),
        "n1": striped(np.random.permutation(S)[:W]),
        "n2": striped(np.random.permutation(S)[:W]),
        "cand": striped(np.random.permutation(T)[:C]),
        "two": striped(np.random.permutation(T)[:S]),
        "k2": striped8(np.random.randint(0, G, (8, H))),
        "n3": striped8(np.stack([np.random.permutation(S) for _ in range(8)])),
        "n4": striped8(np.stack([np.random.permutation(S) for _ in range(8)])),
    }


def reference(x_words, x_scales, d_words, d_scales, gs, tau, offs, k1, n1, n2, cand, two, k2, n3, n4):
    d_k2 = unpack_weight(d_words, d_scales)[np.arange(K)[:, None], runs(k2, K)]
    x_two = unpack_weight(x_words, x_scales)[:, unstriped(two)]
    b = 0.0625 * (d_k2.T @ x_two)
    top = b.max(axis=1, keepdims=True)
    ea = np.exp(f64(tau) * (b[np.arange(H)[:, None], runs(n3, H)] - top))
    x_cand = unpack_weight(x_words, x_scales)[:, unstriped(cand)]
    d_k1 = unpack_weight(d_words, d_scales)[np.arange(K)[:, None], runs(k1, K)]
    xq = unpack_weight(x_words, x_scales)[:, unstriped(offs)]
    h = 0.0625 * (d_k1.T @ xq)
    pa = h[:, unstriped(n2)]
    old = h[:, unstriped(n1)]
    ra = np.minimum(pa, old) - (0.5 * pa)
    ds = h.copy()
    ds[:, unstriped(n1)] = ra
    z = f64(gs) * ds
    a = 0.0625 * ((x_cand.T @ mxq(z, 0, "e4m3")))
    out_0 = (2.0 * ea) * (a - (a[np.arange(C)[:, None], runs(n4, C)])) - (0.5 * b)
    return (out_0,) + planes(out_0)

from contextlib import ExitStack

import concourse.mybir as mybir

F32 = mybir.dt.float32
BF16 = mybir.dt.bfloat16
I32 = mybir.dt.int32
U32 = mybir.dt.uint32
U16 = mybir.dt.uint16
U8 = mybir.dt.uint8
FP8X4 = mybir.dt.float8_e4m3fn_x4
ALU = mybir.AluOpType
ACT = mybir.ActivationFunctionType

P = 128
PACK = 4
K, T, S, G, H, W, C = 512, 1024, 512, 2048, 512, 384, 512
FLOPS = 3 * 2 * 512 * 512 * 512


def tile_picked_pqcjpxbkmin_none_po_kernel(
    tc, x_words, x_scales, d_words, d_scales, gs, tau, offs, k1, n1, n2, cand, two, k2, n3, n4, out_0, out_1, out_2
):
    nc = tc.nc
    with ExitStack() as ctx:
        lists = ctx.enter_context(tc.tile_pool(name="lists", bufs=1))
        keep = ctx.enter_context(tc.tile_pool(name="keep", bufs=1))
        psum = ctx.enter_context(tc.psum_pool(name="psum", bufs=1))

        def load_list(name, src):
            tile = lists.tile([P, src.shape[1]], U16, name=name)
            nc.sync.dma_start(tile[:], src)
            return tile

        def sb(name, shape, dtype, tag=None):
            return keep.tile(shape, dtype, name=name, tag=tag or name, align_bytes=64)

        def dealt(ap):
            return ap.rearrange("p (t m) -> p m t", t=PACK)

        def in_order(ap):
            return ap.rearrange("p (m t) -> p m t", t=PACK)

        d_bytes = sb("d_bytes", [P, G], U8)
        x_bytes = sb("x_bytes", [P, T], U8)
        k1_t = load_list("k1_t", k1)
        nc.sync.dma_start(d_bytes[:].bitcast(I32), d_scales[0].bitcast(I32).unsqueeze(1).to_broadcast([16, 8, G // 4]))
        offs_t = load_list("offs_t", offs)
        x_tab = sb("x_tab", [P, T], U32)
        nc.sync.dma_start(x_tab[:].bitcast(I32), x_words[0].rearrange("p n t -> p (n t)").bitcast(I32))
        d_tab = sb("d_tab", [P, G], U32)
        nc.sync.dma_start(d_tab[:].bitcast(I32), d_words[0].rearrange("p n t -> p (n t)").bitcast(I32))
        for q in range(4):
            x_rows = x_scales[0, 4 * q : 4 * q + 4, :].bitcast(I32)
            nc.scalar.dma_start(x_bytes[32 * q : 32 * q + 32, :].bitcast(I32), x_rows.unsqueeze(0).to_broadcast([8, 4, T // 4]))
        k2_t = load_list("k2_t", k2)
        two_t = load_list("two_t", two)
        n2_t = load_list("n2_t", n2)
        n1_t = load_list("n1_t", n1)
        cand_t = load_list("cand_t", cand)
        n3_t = load_list("n3_t", n3)
        n4_t = load_list("n4_t", n4)
        gs_t = sb("gs_t", [P, PACK], F32)
        nc.sync.dma_start(gs_t[:], gs.rearrange("(p t) o -> p (t o)", t=PACK))
        tau_t = sb("tau_t", [P, PACK], F32)
        nc.sync.dma_start(tau_t[:], tau.rearrange("(p t) o -> p (t o)", t=PACK))

        def code_bytes(name, lst):
            got = sb(name + "_got", [P, H], U8)
            nc.vector.tensor_copy(got[:], d_bytes[:].indirect(lst[:]))
            sorted_b = sb(name + "_dealt", [P, H], U8)
            nc.vector.tensor_copy(dealt(sorted_b[:]), in_order(got[:]))
            placed = sb(name + "_placed", [P, H], U8)
            nc.vector.memset(placed[:].bitcast(I32), 0)
            for q in range(4):
                nc.sync.dma_start(placed[32 * q : 32 * q + 4, :].bitcast(I32), sorted_b[32 * q : 32 * q + 32 : 8, :].bitcast(I32))
            return placed

        def code_words(name, lst, tag=None):
            got = sb(name + "_got", [P, H], U32, tag)
            nc.vector.tensor_copy(got[:], d_tab[:].indirect(lst[:]))
            sorted_w = sb(name + "_dealt", [P, H], U32)
            nc.vector.tensor_copy(dealt(sorted_w[:].bitcast(I32)), in_order(got[:].bitcast(I32)))
            return sorted_w

        def token(name, table, dtype, lst, view, tag=None):
            got = sb(name, [P, S], dtype, tag)
            nc.vector.tensor_copy(view(got[:]), table[:].indirect(lst[:]))
            return got

        def plain(ap):
            return ap

        def product(bank, lw, lb, t, rw, rb):
            cols = slice(P * t, P * (t + 1))
            nc.tensor.matmul_mx(
                out=bank[:], lhsT=lw[:, cols].bitcast(FP8X4), lhsT_scale=lb[:, cols],
                rhs=rw[:].bitcast(FP8X4), rhs_scale=rb[:], start=True, stop=True,
            )

        k1_b = code_bytes("k1_b", k1_t)
        xq_w = token("xq_w", x_tab, U32, offs_t, plain)
        k1_w = code_words("k1_w", k1_t)
        xq_b = token("xq_b", x_bytes, U8, offs_t, plain)
        ds = []
        half_pa = []
        for t in range(PACK):
            bank = psum.tile([P, S], F32, name=f"ha{t}", tag=f"ha{t}")
            product(bank, k1_w, k1_b, t, xq_w, xq_b)
            row = sb(f"ds{t}", [P, S], F32)
            nc.scalar.activation(row[:], bank[:], ACT.Copy, scale=0.0625)
            ds.append(row)
            neg = sb(f"neg{t}", [P, W], F32)
            nc.scalar.activation(neg[:], row[:].indirect(n2_t[:]), ACT.Copy, scale=-0.5)
            half_pa.append(neg)

        pairs = sb("pairs", [P, 2, S, 2], BF16)
        ra = sb("ra", [P, PACK, W], F32)
        for t in range(PACK):
            cand_old = sb(f"cand_old{t}", [P, W], F32)
            nc.vector.tensor_tensor(cand_old[:], ds[t][:].indirect(n1_t[:]), half_pa[t][:], ALU.add)
            nc.vector.scalar_tensor_tensor(ra[:, t, :], half_pa[t][:], -1.0, cand_old[:], ALU.mult, ALU.min)
            nc.scalar.activation(ds[t][:].indirect(n1_t[:]), ra[:, t, :], ACT.Copy)

        k2_b = code_bytes("k2_b", k2_t)
        two_w = token("two_w", x_tab, U32, two_t, plain)
        two_b = token("two_b", x_bytes, U8, two_t, plain)
        k2_w = code_words("k2_w", k2_t, "cand_old0")
        cand_w = token("cand_w", x_tab, U32, cand_t, dealt, "cand_old1")
        cand_b = token("cand_b", x_bytes, U8, cand_t, dealt, "cand_old2")
        top = sb("top", [P, PACK], F32)
        b_banks = []
        b_rows = []
        for t in range(PACK):
            bank = psum.tile([P, S], F32, name=f"b{t}", tag=f"b{t}")
            product(bank, k2_w, k2_b, t, two_w, two_b)
            row = sb(f"b_row{t}", [P, S], F32)
            nc.vector.tensor_scalar(row[:], bank[:], 0.0625, None, ALU.mult, ALU.max, accum_out=top[:, t : t + 1])
            b_banks.append(bank)
            b_rows.append(row)
        bias = sb("bias", [P, PACK], F32)
        nc.vector.scalar_tensor_tensor(bias[:], top[:], -1.0, tau_t[:], ALU.mult, ALU.mult)

        for t in range(PACK):
            nc.vector.tensor_scalar(pairs[:, t // 2, :, t % 2], ds[t][:], gs_t[:, t : t + 1], None, ALU.mult)
        z_in = sb("z_in", [P, S * PACK], BF16)
        z_words = z_in[:].bitcast(F32).rearrange("p (c u) -> p c u", u=2)
        pair_words = pairs[:].rearrange("p u c e -> p (u c e)").bitcast(F32).rearrange("p (u c) -> p c u", u=2)
        nc.vector.tensor_copy(z_words, pair_words)
        z_w = sb("z_w", [P, S], U32)
        z_b = sb("z_b", [P, S], U8)
        nc.vector.quantize_mx(out=z_w[:].bitcast(FP8X4), scales=z_b[:], in_=z_in[:])

        def rate(t, dst):
            for lo in (0, 256):
                nc.scalar.activation(
                    dst[:, lo : lo + 256], b_rows[t][:].indirect(n3_t[:, lo // 16 : lo // 16 + 16]), ACT.Exp,
                    bias=bias[:, t : t + 1], scale=tau_t[:, t : t + 1],
                )

        ea_early = sb("ea_early", [P, 3, S], F32, tag="ra")
        ea = [ea_early[:, t, :] for t in range(3)]
        for t in range(3):
            rate(t, ea[t])

        a_banks = []
        a_rows = []
        for t in range(PACK):
            bank = psum.tile([P, S], F32, name=f"a{t}", tag=f"ha{t}")
            product(bank, cand_w, cand_b, t, z_w, z_b)
            row = sb(f"a_row{t}", [P, S], F32)
            nc.vector.tensor_scalar(row[:], bank[:], 0.0625, None, ALU.mult)
            a_banks.append(bank)
            a_rows.append(row)

        y = sb("y", [P, PACK, S], F32)
        y_in = sb("y_in", [P, S, 2, 2], BF16)
        y_w = sb("y_w", [P, S], U32)
        y_b = sb("y_b", [P, S], U8)
        far = sb("far", [P, PACK, S], F32)
        diff = sb("diff", [P, PACK, S], F32)
        prod = sb("prod", [P, PACK, S], F32)
        out_rows = out_0.rearrange("(p t) c -> p t c", t=PACK)
        out_words = out_1[0].rearrange("p n t -> p (n t)").bitcast(I32)
        for t in range(PACK):
            if t == PACK - 1:
                ea_late = sb("ea_late", [P, S], F32, tag="a_row1")
                ea.append(ea_late[:])
                rate(t, ea[t])
            for lo in (0, 256):
                nc.scalar.activation(far[:, t, lo : lo + 256], a_rows[t][:].indirect(n4_t[:, lo // 16 : lo // 16 + 16]), ACT.Copy)
            nc.vector.scalar_tensor_tensor(diff[:, t, :], a_banks[t][:], 0.0625, far[:, t, :], ALU.mult, ALU.subtract)
            nc.vector.scalar_tensor_tensor(prod[:, t, :], diff[:, t, :], 2.0, ea[t], ALU.mult, ALU.mult)
            nc.vector.scalar_tensor_tensor(y[:, t, :], b_banks[t][:], -0.03125, prod[:, t, :], ALU.mult, ALU.add)
            nc.sync.dma_start(out_rows[:, t, :], y[:, t, :])
        nc.scalar.copy(y_in[:, :, 0, :], y[:, 0:2, :].rearrange("p t c -> p c t"))
        for lo in (0, 256):
            hi = lo + 256
            nc.vector.tensor_copy(y_in[:, lo:hi, 1, :], y[:, 2:4, lo:hi].rearrange("p t c -> p c t"))
            nc.vector.quantize_mx(
                out=y_w[:, lo:hi].bitcast(FP8X4), scales=y_b[:, lo:hi], in_=y_in[:, lo:hi, :, :].rearrange("p c u e -> p (c u e)")
            )
            nc.sync.dma_start(out_words[:, lo:hi], y_w[:, lo:hi].bitcast(I32))
        for q in range(4):
            nc.scalar.dma_start(out_2[0, 4 * q : 4 * q + 4, :].bitcast(I32), y_b[32 * q : 32 * q + 4, :].bitcast(I32))
